import numpy as np
import ml_dtypes


def mxq(x, axis, fmt="e4m3"):
    dtype, down = {"e4m3": (ml_dtypes.float8_e4m3fn, 7), "e5m2": (ml_dtypes.float8_e5m2, 14)}[fmt]
    v = np.moveaxis(np.asarray(x, np.float32).astype(ml_dtypes.bfloat16).astype(np.float64), axis, -1)
    blocks = v.reshape(v.shape[:-1] + (-1, 32))
    amax = np.abs(blocks).max(-1, keepdims=True)
    byte = np.maximum(np.where(amax > 0, np.frexp(amax)[1] - 1 + 127, 0) - down, 1)
    scale = np.exp2(byte - 127.0)
    codes = (blocks / scale).astype(np.float32).astype(dtype).astype(np.float64)
    return np.moveaxis((codes * scale).reshape(v.shape), -1, axis)


WIDE = False


def mx_kscale(k):
    if not WIDE:
        return np.ones(k)
    levels = np.array([10, -10, 5, -5, 0])
    if k % 512:
        return np.exp2(np.random.permutation(np.resize(levels, k // 32))).repeat(32)
    a = np.empty((k // 512, 16))
    for p in range(k // 512):
        a[p, :8] = np.random.permutation(np.resize(levels, 8))
        for g in range(8):
            far = levels[np.abs(levels - a[p, g]) >= 10]
            a[p, g + 8] = far[np.random.randint(len(far))]
    return np.exp2(a.ravel()).repeat(32)


BF16 = ml_dtypes.bfloat16


def bf(x):
    return np.asarray(x, np.float32).astype(BF16)


def f64(x):
    return np.asarray(x).astype(np.float64)


E2M1 = np.array([0.0, 0.5, 1.0, 1.5, 2.0, 3.0, 4.0, 6.0, -0.0, -0.5, -1.0, -1.5, -2.0, -3.0, -4.0, -6.0])


def pack_weight(w, fmt):
    k, n = w.shape
    w = f64(bf(w)).reshape(k // 32, 32, n)
    amax = np.abs(w).max(1)
    if fmt == "e4m3":
        byte = np.frexp(amax)[1] - 1 + 127 - 7
    else:
        mant, ex = np.frexp(amax / 6.0)
        byte = np.where(mant > 0.5, ex, ex - 1) + 127
    byte = np.clip(np.where(amax > 0, byte, 1), 1, 254)
    scaled = (w * np.exp2(127.0 - byte)[:, None, :]).reshape(k, n).astype(np.float32)
    by_word = np.ascontiguousarray(scaled.reshape(k // 512, 128, 4, n).transpose(0, 1, 3, 2))
    if fmt == "e4m3":
        words = by_word.astype(ml_dtypes.float8_e4m3fn).view(np.uint8)
    else:
        c = by_word.astype(ml_dtypes.float4_e2m1fn).view(np.uint8) & 0xF
        words = c[..., 0::2] | (c[..., 1::2] << 4)
    return np.ascontiguousarray(words), np.ascontiguousarray(byte.astype(np.uint8).reshape(k // 512, 16, n))


def unpack_weight(words, scales, fmt):
    g, p, n, _ = words.shape
    if fmt == "e4m3":
        vals = np.ascontiguousarray(words).view(ml_dtypes.float8_e4m3fn).astype(np.float64)
    else:
        nib = np.empty((g, p, n, 4), np.uint8)
        nib[..., 0::2] = words & 0xF
        nib[..., 1::2] = words >> 4
        vals = E2M1[nib]
    vals = vals * np.repeat(np.exp2(scales.astype(np.float64) - 127.0), 8, axis=1)[..., None]
    return vals.transpose(0, 1, 3, 2).reshape(g * 512, n)
def pack4(w):
    words, scales = pack_weight(w, "e2m1")
    return words.reshape(words.shape[0], 128, -1), scales


def unpack4(words, scales):
    return unpack_weight(words.reshape(words.shape[0], 128, -1, 2), scales, "e2m1")


C, S, B, A = 4, 1024, 512, 1024


def setup_inputs():
    s = mx_kscale(C * B)
    t = mx_kscale(C * A)
    h = np.random.standard_normal((C, B, A)) / (B * A) ** 0.25
    sell = h.reshape(C * B, A) / s[:, None]
    hold = h.transpose(0, 2, 1).reshape(C * A, B) / t[:, None]
    sell_words, sell_scales = pack4(sell)
    hold_words, hold_scales = pack4(hold)
    return {"loss": bf(np.random.standard_normal((C, S, B))),
            "lev": bf(np.exp(0.3 * np.random.standard_normal((C, B))) * s.reshape(C, B)),
            "impact": bf(np.exp(0.3 * np.random.standard_normal((C, A))) * t.reshape(C, A)),
            "sell_words": sell_words, "sell_scales": sell_scales,
            "hold_words": hold_words, "hold_scales": hold_scales}


def reference(loss, lev, impact, sell_words, sell_scales, hold_words, hold_scales):
    sell = unpack4(sell_words, sell_scales).reshape(C, B, A)
    hold = unpack4(hold_words, hold_scales).reshape(C, A, B)
    liq = f64(loss) * f64(lev)[:, None, :]
    sales = mxq(liq, 2, "e4m3") @ sell
    drop = np.maximum(sales, 0.0) * f64(impact)[:, None, :]
    return mxq(drop, 2, "e4m3") @ hold

@@ -1,0 +1,356 @@
+from contextlib import ExitStack
+
+import concourse.mybir as mybir
+from concourse.masks import make_identity
+
+C, S, B, A = 4, 1024, 512, 1024
+FLOPS = 2 * C * S * B * A * 2
+
+F32 = mybir.dt.float32
+BF16 = mybir.dt.bfloat16
+I32 = mybir.dt.int32
+U32 = mybir.dt.uint32
+U8 = mybir.dt.uint8
+FP8X4 = mybir.dt.float8_e4m3fn_x4
+FP4X4 = mybir.dt.float4_e2m1fn_x4
+ACT = mybir.ActivationFunctionType
+ALU = mybir.AluOpType
+
+P = 128
+PACK = 4
+K_PASS = P * PACK
+GROUPS = A // K_PASS
+ROWS = 512
+HALVES = S // ROWS
+BLOCKS = C * HALVES
+SLOT_ORDER = (0, 2, 1, 3)
+SCALAR_COLS = [(512, 256)] * 5 + [(512, 0)] * 3
+
+
+def tile_fire_sale_contagion_s14_kernel(
+    tc, loss, lev, impact, sell_words, sell_scales, hold_words, hold_scales, out
+):
+    nc = tc.nc
+    with ExitStack() as ctx:
+        keep = ctx.enter_context(tc.tile_pool(name="keep", bufs=1))
+        work = ctx.enter_context(tc.tile_pool(name="work", bufs=2))
+        psum_v = ctx.enter_context(tc.psum_pool(name="psum_v", bufs=4))
+        psum_s = ctx.enter_context(tc.psum_pool(name="psum_s", bufs=4))
+        ctx.enter_context(tc.manual_schedule())
+
+        ident = keep.tile([P, P], F32, name="ident")
+        make_identity(nc, ident[:])
+
+        sell_scale_first = keep.tile([P, A], U8, name="sell_scale_first", align_bytes=64)
+        sell_scale_rest = keep.tile([P, C - 1, A], U8, name="sell_scale_rest", align_bytes=64)
+        hold_scale = keep.tile([P, C * GROUPS, B], U8, name="hold_scale", align_bytes=64)
+        nc.vector.memset(sell_scale_first[:].bitcast(I32), 0)
+        nc.vector.memset(sell_scale_rest[:].bitcast(I32), 0)
+        nc.vector.memset(hold_scale[:].bitcast(I32), 0)
+
+        lev_t = keep.tile([P, C, PACK], BF16, name="lev_t")
+        imp_t = keep.tile([P, C, GROUPS, PACK], BF16, name="imp_t")
+        nc.scalar.dma_start(out=lev_t[:], in_=lev.rearrange("c (p t) -> p c t", t=PACK))
+        nc.scalar.dma_start(
+            out=imp_t[:].rearrange("p c g t -> p (c g) t"),
+            in_=impact.rearrange("c (g p t) -> p (c g) t", g=GROUPS, t=PACK),
+        )
+        imp_abs = keep.tile([P, C, GROUPS, PACK], F32, name="imp_abs")
+        imp_sign = keep.tile([P, C, GROUPS, PACK], BF16, name="imp_sign")
+        nc.scalar.activation(out=imp_abs[:], in_=imp_t[:], func=ACT.Abs)
+        nc.scalar.activation(out=imp_sign[:], in_=imp_t[:], func=ACT.Sign)
+
+        loss_rows = {}
+        sell_raw = {}
+        hold_code = {}
+
+        def load_loss(i, part):
+            c, h = divmod(i, HALVES)
+            rows = loss[c, h * ROWS : (h + 1) * ROWS, :].rearrange("(p j) b -> p j b", j=PACK)
+            t = keep.tile([P, 2, B], BF16, name="loss_%d_%d" % (i, part))
+            nc.sync.dma_start(out=t[:], in_=rows[:, 2 * part : 2 * part + 2, :])
+            loss_rows[i, part] = t
+
+        def load_sell(c, g):
+            t = keep.tile([P, 2 * K_PASS], U8, name="sell_raw_%d_%d" % (c, g), align_bytes=64)
+            nc.sync.dma_start(
+                out=t[:].bitcast(I32), in_=sell_words[c, :, 2 * K_PASS * g : 2 * K_PASS * (g + 1)].bitcast(I32)
+            )
+            sell_raw[c, g] = t
+
+        def load_hold(c):
+            t = keep.tile([P, GROUPS, 2 * B], U8, name="hold_code_%d" % c, align_bytes=64)
+            nc.sync.dma_start(
+                out=t[:].bitcast(I32),
+                in_=hold_words[GROUPS * c : GROUPS * (c + 1)].rearrange("g p n -> p g n").bitcast(I32),
+            )
+            hold_code[c] = t
+
+        load_loss(0, 0)
+        load_sell(0, 0)
+        for q in range(4):
+            nc.sync.dma_start(
+                out=sell_scale_first[32 * q : 32 * q + 4, :].bitcast(I32),
+                in_=sell_scales[0, 4 * q : 4 * q + 4, :].bitcast(I32),
+            )
+        load_loss(0, 1)
+        load_sell(0, 1)
+        load_loss(1, 0)
+        load_loss(1, 1)
+        load_hold(0)
+        for q in range(4):
+            nc.sync.dma_start(
+                out=hold_scale[32 * q : 32 * q + 4, :, :].bitcast(I32),
+                in_=hold_scales[:, 4 * q : 4 * q + 4, :].rearrange("g r n -> r g n").bitcast(I32),
+            )
+        for q in range(4):
+            nc.sync.dma_start(
+                out=sell_scale_rest[32 * q : 32 * q + 4, :, :].bitcast(I32),
+                in_=sell_scales[1:C, 4 * q : 4 * q + 4, :].rearrange("c r n -> r c n").bitcast(I32),
+            )
+        for c in range(1, C):
+            load_sell(c, 0)
+            load_sell(c, 1)
+            for i in range(HALVES * c, HALVES * (c + 1)):
+                load_loss(i, 0)
+                load_loss(i, 1)
+            load_hold(c)
+
+        sell_code = {}
+        sell_scale = {}
+
+        def sort_codes(c, g):
+            code = keep.tile([P, PACK, 2 * P], U8, name="sell_code_%d_%d" % (c, g), align_bytes=64)
+            nc.vector.tensor_copy(
+                out=code[:].rearrange("p t (m b) -> p t m b", b=2),
+                in_=sell_raw[c, g][:].rearrange("p (m t b) -> p t m b", t=PACK, b=2),
+            )
+            sell_code[c, g] = code
+
+        def sort_scales(c, g):
+            scale = keep.tile([P, PACK, P], U8, name="sell_scale_%d_%d" % (c, g), align_bytes=64)
+            raw_scale = sell_scale_first[:] if c == 0 else sell_scale_rest[:, c - 1, :]
+            nc.vector.tensor_copy(
+                out=scale[:],
+                in_=raw_scale[:, K_PASS * g : K_PASS * (g + 1)].rearrange("p (m t) -> p t m", t=PACK),
+            )
+            sell_scale[c, g] = scale
+
+        liq = {}
+        liq_code = {}
+        liq_scale = {}
+
+        def new_liq(i):
+            liq[i] = work.tile([P, ROWS, PACK], BF16, name="liq", tag="liq", align_bytes=64)
+            liq_code[i] = work.tile([P, ROWS], U32, name="liq_code", tag="liq_code", align_bytes=64)
+            liq_scale[i] = work.tile([P, ROWS], U8, name="liq_scale", tag="liq_scale", align_bytes=64)
+
+        turned = {}
+
+        def turn_loss(i, part):
+            turned[i, part] = psum_v.tile([P, 2, 2 * P], F32, name="turned", tag="bank")
+            for j in range(2):
+                words = loss_rows[i, part][:, j, :].bitcast(F32)
+                for u in range(2):
+                    nc.tensor.transpose(turned[i, part][:, u, j * P : (j + 1) * P], words[:, u : 2 * P : 2], ident[:])
+
+        def leverage(i, part):
+            c = i // HALVES
+            nc.vector.tensor_tensor(
+                out=liq[i][:, 2 * P * part : 2 * P * (part + 1), :].rearrange("p s (u e) -> p s u e", e=2),
+                in0=turned[i, part][:].bitcast(BF16).rearrange("p u (s e) -> p s u e", e=2),
+                in1=lev_t[:, c : c + 1, :].rearrange("p o (u e) -> p o u e", e=2).broadcast_to([P, 2 * P, 2, 2]),
+                op=ALU.mult,
+            )
+
+        def quantize_liq(i, s0, width):
+            nc.vector.quantize_mx(
+                out=liq_code[i][:, s0 : s0 + width].bitcast(FP8X4),
+                scales=liq_scale[i][:, s0 : s0 + width],
+                in_=liq[i][:, s0 : s0 + width, :].rearrange("p s t -> p (s t)"),
+            )
+
+        def sales(dst, i, g, t, s0, width):
+            c = i // HALVES
+            nc.tensor.matmul_mx(
+                out=dst,
+                lhsT=sell_code[c, g][:, t, :].bitcast(FP4X4),
+                lhsT_scale=sell_scale[c, g][:, t, :],
+                rhs=liq_code[i][:, s0 : s0 + width].bitcast(FP8X4),
+                rhs_scale=liq_scale[i][:, s0 : s0 + width],
+                start=True,
+                stop=True,
+            )
+
+        pairs = {}
+        drop = {}
+        drop_code = {}
+        drop_scale = {}
+
+        def new_drop(i, g):
+            drop[i, g] = work.tile([P, ROWS, PACK], BF16, name="drop", tag="drop", bufs=4, align_bytes=64)
+            drop_code[i, g] = work.tile([P, ROWS], U32, name="drop_code", tag="drop_code", bufs=4, align_bytes=64)
+            drop_scale[i, g] = work.tile([P, ROWS], U8, name="drop_scale", tag="drop_scale", bufs=4, align_bytes=64)
+
+        def new_pairs(i, g):
+            pairs[i, g] = work.tile([P, 2, ROWS, 2], BF16, name="pairs", tag="pairs", bufs=3, align_bytes=64)
+
+        def scalar_bank(i, g, n, s0, width):
+            c = i // HALVES
+            per_bank = ROWS // width
+            bank = psum_s.tile([P, per_bank, width], F32, name="sales_s", tag="bank")
+            slots = SLOT_ORDER[n * per_bank : (n + 1) * per_bank]
+            for k, t in enumerate(slots):
+                sales(bank[:, k, :], i, g, t, s0, width)
+            for k, t in enumerate(slots):
+                nc.scalar.activation(
+                    out=pairs[i, g][:, t // 2, s0 : s0 + width, t % 2],
+                    in_=bank[:, k, :],
+                    func=ACT.Relu,
+                    scale=imp_abs[:, c, g, t : t + 1],
+                )
+
+        def join_pairs(i, g, s0, width):
+            c = i // HALVES
+            nc.vector.tensor_tensor(
+                out=drop[i, g][:, s0 : s0 + width, :].rearrange("p s (u e) -> p s u e", e=2),
+                in0=pairs[i, g][:, :, s0 : s0 + width, :].rearrange("p u s e -> p s u e"),
+                in1=imp_sign[:, c, g : g + 1, :].rearrange("p o (u e) -> p o u e", e=2).broadcast_to([P, width, 2, 2]),
+                op=ALU.mult,
+            )
+
+        def vector_bank(i, g, s0):
+            c = i // HALVES
+            bank = psum_v.tile([P, PACK, P], F32, name="sales_v", tag="bank")
+            for t in range(PACK):
+                sales(bank[:, t, :], i, g, t, s0, P)
+            nc.vector.scalar_tensor_tensor(
+                out=drop[i, g][:, s0 : s0 + P, :],
+                in0=bank[:].rearrange("p t s -> p s t"),
+                scalar=0.0,
+                in1=imp_t[:, c, g : g + 1, :].broadcast_to([P, P, PACK]),
+                op0=ALU.max,
+                op1=ALU.mult,
+            )
+
+        def quantize_drop(i, g, s0, width):
+            nc.vector.quantize_mx(
+                out=drop_code[i, g][:, s0 : s0 + width].bitcast(FP8X4),
+                scales=drop_scale[i, g][:, s0 : s0 + width],
+                in_=drop[i, g][:, s0 : s0 + width, :].rearrange("p s t -> p (s t)"),
+            )
+
+        def losses(i, j):
+            c = i // HALVES
+            cols = slice(j * P, (j + 1) * P)
+            bank = psum_s.tile([P, B], F32, name="acc", tag="bank")
+            for g in range(GROUPS):
+                nc.tensor.matmul_mx(
+                    out=bank[:],
+                    lhsT=drop_code[i, g][:, cols].bitcast(FP8X4),
+                    lhsT_scale=drop_scale[i, g][:, cols],
+                    rhs=hold_code[c][:, g, :].bitcast(FP4X4),
+                    rhs_scale=hold_scale[:, GROUPS * c + g, :],
+                    start=(g == 0),
+                    stop=(g == GROUPS - 1),
+                )
+            return bank
+
+        def out_rows(i):
+            c, h = divmod(i, HALVES)
+            return out[c, h * ROWS : (h + 1) * ROWS, :].rearrange("(p j) b -> p j b", j=PACK)
+
+        def second_round(i, part):
+            result = work.tile([P, 2, B], F32, name="result", tag="result", bufs=8)
+            for j in range(2):
+                nc.scalar.copy(out=result[:, j, :], in_=losses(i, 2 * part + j)[:])
+            nc.sync.dma_start(out=out_rows(i)[:, 2 * part : 2 * part + 2, :], in_=result[:])
+
+        half = ROWS // 2
+        last = BLOCKS - 1
+
+        new_liq(0)
+        new_pairs(0, 0)
+        turn_loss(0, 0)
+        sort_codes(0, 0)
+        leverage(0, 0)
+        turn_loss(0, 1)
+        sort_scales(0, 0)
+        quantize_liq(0, 0, half)
+        scalar_bank(0, 0, 0, 0, half)
+        scalar_bank(0, 0, 1, 0, half)
+        leverage(0, 1)
+        sort_scales(0, 1)
+        quantize_liq(0, half, half)
+        sort_codes(0, 1)
+        for i in range(last):
+            c, h = divmod(i, HALVES)
+            width = SCALAR_COLS[i][1]
+            new_drop(i, 0)
+            new_liq(i + 1)
+            if i == 0:
+                turn_loss(1, 0)
+                turn_loss(1, 1)
+                scalar_bank(0, 0, 0, half, half)
+                scalar_bank(0, 0, 1, half, half)
+            else:
+                new_pairs(i, 0)
+                scalar_bank(i, 0, 0, 0, ROWS)
+                scalar_bank(i, 0, 1, 0, ROWS)
+                turn_loss(i + 1, 0)
+                turn_loss(i + 1, 1)
+            leverage(i + 1, 0)
+            leverage(i + 1, 1)
+            if i > 0:
+                quantize_drop(i - 1, 1, 0, ROWS)
+                scalar_bank(i, 0, 2, 0, ROWS)
+                scalar_bank(i, 0, 3, 0, ROWS)
+            if c + 1 < C:
+                sort_scales(c + 1, h)
+            quantize_liq(i + 1, 0, ROWS)
+            new_drop(i, 1)
+            if c + 1 < C:
+                sort_codes(c + 1, h)
+            join_pairs(i, 0, 0, ROWS)
+            for s0 in range(width, ROWS, P):
+                vector_bank(i, 1, s0)
+            if width:
+                new_pairs(i, 1)
+                for n in range(PACK * width // ROWS):
+                    scalar_bank(i, 1, n, 0, width)
+            quantize_drop(i, 0, 0, ROWS)
+            if i > 0:
+                second_round(i - 1, 0)
+                second_round(i - 1, 1)
+            if width:
+                join_pairs(i, 1, 0, width)
+
+        def final_rows(j, engine_copy):
+            result = work.tile([P, B], F32, name="result", tag="result", bufs=8)
+            engine_copy(out=result[:], in_=losses(last, j)[:])
+            nc.sync.dma_start(out=out_rows(last)[:, j, :], in_=result[:])
+
+        new_pairs(last, 0)
+        new_drop(last, 0)
+        new_drop(last, 1)
+        scalar_bank(last, 0, 0, 0, half)
+        scalar_bank(last, 0, 1, 0, half)
+        vector_bank(last, 1, 0)
+        quantize_drop(last - 1, 1, 0, ROWS)
+        vector_bank(last, 1, P)
+        scalar_bank(last, 0, 0, half, half)
+        scalar_bank(last, 0, 1, half, half)
+        join_pairs(last, 0, 0, half)
+        quantize_drop(last, 1, 0, half)
+        vector_bank(last, 1, 2 * P)
+        quantize_drop(last, 0, 0, half)
+        vector_bank(last, 1, 3 * P)
+        second_round(last - 1, 0)
+        join_pairs(last, 0, half, half)
+        quantize_drop(last, 1, half, half)
+        second_round(last - 1, 1)
+        quantize_drop(last, 0, half, half)
+        final_rows(0, nc.scalar.copy)
+        final_rows(1, nc.vector.tensor_copy)
+        final_rows(2, nc.scalar.copy)
+        final_rows(3, nc.vector.tensor_copy)

@@ -24,7 +24,7 @@ ROWS = 512
 HALVES = S // ROWS
 BLOCKS = C * HALVES
 SLOT_ORDER = (0, 2, 1, 3)
-SCALAR_COLS = [(512, 256)] * 5 + [(512, 0)] * 3
+SCALAR_COLS = [(512, 256)] + [(512, 128)] * 6 + [(512, 0)]
 
 
 def tile_fire_sale_contagion_s14_kernel(
@@ -37,28 +37,6 @@ def tile_fire_sale_contagion_s14_kernel(
         psum_v = ctx.enter_context(tc.psum_pool(name="psum_v", bufs=4))
         psum_s = ctx.enter_context(tc.psum_pool(name="psum_s", bufs=4))
         ctx.enter_context(tc.manual_schedule())
-
-        ident = keep.tile([P, P], F32, name="ident")
-        make_identity(nc, ident[:])
-
-        sell_scale_first = keep.tile([P, A], U8, name="sell_scale_first", align_bytes=64)
-        sell_scale_rest = keep.tile([P, C - 1, A], U8, name="sell_scale_rest", align_bytes=64)
-        hold_scale = keep.tile([P, C * GROUPS, B], U8, name="hold_scale", align_bytes=64)
-        nc.vector.memset(sell_scale_first[:].bitcast(I32), 0)
-        nc.vector.memset(sell_scale_rest[:].bitcast(I32), 0)
-        nc.vector.memset(hold_scale[:].bitcast(I32), 0)
-
-        lev_t = keep.tile([P, C, PACK], BF16, name="lev_t")
-        imp_t = keep.tile([P, C, GROUPS, PACK], BF16, name="imp_t")
-        nc.scalar.dma_start(out=lev_t[:], in_=lev.rearrange("c (p t) -> p c t", t=PACK))
-        nc.scalar.dma_start(
-            out=imp_t[:].rearrange("p c g t -> p (c g) t"),
-            in_=impact.rearrange("c (g p t) -> p (c g) t", g=GROUPS, t=PACK),
-        )
-        imp_abs = keep.tile([P, C, GROUPS, PACK], F32, name="imp_abs")
-        imp_sign = keep.tile([P, C, GROUPS, PACK], BF16, name="imp_sign")
-        nc.scalar.activation(out=imp_abs[:], in_=imp_t[:], func=ACT.Abs)
-        nc.scalar.activation(out=imp_sign[:], in_=imp_t[:], func=ACT.Sign)
 
         loss_rows = {}
         sell_raw = {}
@@ -88,53 +66,79 @@ def tile_fire_sale_contagion_s14_kernel(
 
         load_loss(0, 0)
         load_sell(0, 0)
+        load_loss(0, 1)
+        lev_first = keep.tile([P, 1, PACK], BF16, name="lev_first")
+        nc.sync.dma_start(out=lev_first[:, 0, :], in_=lev[0].rearrange("(p t) -> p t", t=PACK))
+
+        ident = keep.tile([P, P], F32, name="ident")
+        make_identity(nc, ident[:])
+
+        factor_rows = keep.tile([P, K_PASS], BF16, name="factor_rows")
+        sell_scale_raw = keep.tile([P, A], U8, name="sell_scale_raw", align_bytes=64)
+        sell_scale_rest = keep.tile([P, C - 1, A], U8, name="sell_scale_rest", align_bytes=64)
+        hold_scale = keep.tile([P, C * GROUPS, B], U8, name="hold_scale", align_bytes=64)
+        nc.vector.memset(sell_scale_raw[:].bitcast(I32), 0)
+        nc.vector.memset(factor_rows[:], 0.0)
+        nc.vector.memset(sell_scale_rest[:].bitcast(I32), 0)
+        nc.vector.memset(hold_scale[:].bitcast(I32), 0)
+
         for q in range(4):
             nc.sync.dma_start(
-                out=sell_scale_first[32 * q : 32 * q + 4, :].bitcast(I32),
-                in_=sell_scales[0, 4 * q : 4 * q + 4, :].bitcast(I32),
+                out=sell_scale_raw[32 * q : 32 * q + 4 * C, :].bitcast(I32),
+                in_=sell_scales[:, 4 * q : 4 * q + 4, :].bitcast(I32),
             )
-        load_loss(0, 1)
+        nc.sync.dma_start(out=factor_rows[0:C, :], in_=lev)
+        nc.sync.dma_start(
+            out=factor_rows[C : C + C * GROUPS, :], in_=impact.rearrange("c (g k) -> (c g) k", g=GROUPS)
+        )
         load_sell(0, 1)
         load_loss(1, 0)
         load_loss(1, 1)
+        load_sell(1, 0)
+        load_sell(1, 1)
         load_hold(0)
         for q in range(4):
             nc.sync.dma_start(
                 out=hold_scale[32 * q : 32 * q + 4, :, :].bitcast(I32),
                 in_=hold_scales[:, 4 * q : 4 * q + 4, :].rearrange("g r n -> r g n").bitcast(I32),
             )
-        for q in range(4):
-            nc.sync.dma_start(
-                out=sell_scale_rest[32 * q : 32 * q + 4, :, :].bitcast(I32),
-                in_=sell_scales[1:C, 4 * q : 4 * q + 4, :].rearrange("c r n -> r c n").bitcast(I32),
-            )
-        for c in range(1, C):
-            load_sell(c, 0)
-            load_sell(c, 1)
-            for i in range(HALVES * c, HALVES * (c + 1)):
-                load_loss(i, 0)
-                load_loss(i, 1)
-            load_hold(c)
+
+        def later_loads():
+            for c in range(1, C):
+                for q in range(4):
+                    nc.sync.dma_start(
+                        out=sell_scale_rest[32 * q : 32 * q + 4, c - 1, :].bitcast(I32),
+                        in_=sell_scale_all[32 * q + 4 * c : 32 * q + 4 * c + 4, :].bitcast(I32),
+                    )
+                if c > 1:
+                    load_sell(c, 0)
+                    load_sell(c, 1)
+                for i in range(HALVES * c, HALVES * (c + 1)):
+                    load_loss(i, 0)
+                    load_loss(i, 1)
+                load_hold(c)
 
         sell_code = {}
-        sell_scale = {}
+        sell_scale_all = keep.tile([P, A], U8, name="sell_scale_all", align_bytes=64)
 
         def sort_codes(c, g):
             code = keep.tile([P, PACK, 2 * P], U8, name="sell_code_%d_%d" % (c, g), align_bytes=64)
             nc.vector.tensor_copy(
-                out=code[:].rearrange("p t (m b) -> p t m b", b=2),
-                in_=sell_raw[c, g][:].rearrange("p (m t b) -> p t m b", t=PACK, b=2),
+                out=code[:].rearrange("p t (w m b) -> p w t m b", m=8, b=2),
+                in_=sell_raw[c, g][:].rearrange("p (w m t b) -> p w t m b", m=8, t=PACK, b=2),
             )
             sell_code[c, g] = code
 
-        def sort_scales(c, g):
-            scale = keep.tile([P, PACK, P], U8, name="sell_scale_%d_%d" % (c, g), align_bytes=64)
-            raw_scale = sell_scale_first[:] if c == 0 else sell_scale_rest[:, c - 1, :]
+        def sort_scales(g):
+            cols = slice(K_PASS * g, K_PASS * (g + 1))
             nc.vector.tensor_copy(
-                out=scale[:],
-                in_=raw_scale[:, K_PASS * g : K_PASS * (g + 1)].rearrange("p (m t) -> p t m", t=PACK),
+                out=sell_scale_all[:, cols].rearrange("p (t w m) -> p w t m", t=PACK, m=16),
+                in_=sell_scale_raw[:, cols].rearrange("p (w m t) -> p w t m", m=16, t=PACK),
             )
-            sell_scale[c, g] = scale
+
+        def sell_scale(c, g, t):
+            plane = sell_scale_all[:] if c == 0 else sell_scale_rest[:, c - 1, :]
+            return plane[:, K_PASS * g + P * t : K_PASS * g + P * (t + 1)]
 
         liq = {}
         liq_code = {}
@@ -156,10 +160,11 @@ def tile_fire_sale_contagion_s14_kernel(
 
         def leverage(i, part):
             c = i // HALVES
+            factor = lev_first[:] if i == 0 else factors[:, c : c + 1, :]
             nc.vector.tensor_tensor(
                 out=liq[i][:, 2 * P * part : 2 * P * (part + 1), :].rearrange("p s (u e) -> p s u e", e=2),
                 in0=turned[i, part][:].bitcast(BF16).rearrange("p u (s e) -> p s u e", e=2),
-                in1=lev_t[:, c : c + 1, :].rearrange("p o (u e) -> p o u e", e=2).broadcast_to([P, 2 * P, 2, 2]),
+                in1=factor.rearrange("p o (u e) -> p o u e", e=2).broadcast_to([P, 2 * P, 2, 2]),
                 op=ALU.mult,
             )
 
@@ -175,7 +180,7 @@ def tile_fire_sale_contagion_s14_kernel(
             nc.tensor.matmul_mx(
                 out=dst,
                 lhsT=sell_code[c, g][:, t, :].bitcast(FP4X4),
-                lhsT_scale=sell_scale[c, g][:, t, :],
+                lhsT_scale=sell_scale(c, g, t),
                 rhs=liq_code[i][:, s0 : s0 + width].bitcast(FP8X4),
                 rhs_scale=liq_scale[i][:, s0 : s0 + width],
                 start=True,
@@ -272,48 +277,63 @@ def tile_fire_sale_contagion_s14_kernel(
         new_liq(0)
         new_pairs(0, 0)
         turn_loss(0, 0)
-        sort_codes(0, 0)
-        leverage(0, 0)
         turn_loss(0, 1)
-        sort_scales(0, 0)
+        n_rows = C + C * GROUPS
+        factor_bank = psum_s.tile([P, 2, P], F32, name="factor_bank", tag="bank")
+        for u in range(2):
+            nc.tensor.transpose(factor_bank[:, u, :], factor_rows[:].bitcast(F32)[:, u : 2 * P : 2], ident[:])
+        factors = keep.tile([P, n_rows, PACK], BF16, name="factors")
+        nc.scalar.copy(out=factors[:].bitcast(F32), in_=factor_bank[:, :, 0:n_rows].rearrange("p u r -> p r u"))
+        imp_t = factors[:, C:n_rows, :].rearrange("p (c g) t -> p c g t", g=GROUPS)
+        imp_abs = keep.tile([P, C, GROUPS, PACK], F32, name="imp_abs")
+        imp_sign = keep.tile([P, C, GROUPS, PACK], BF16, name="imp_sign")
+        nc.scalar.activation(out=imp_abs[:], in_=imp_t, func=ACT.Abs)
+        nc.scalar.activation(out=imp_sign[:], in_=imp_t, func=ACT.Sign)
+
+        sort_codes(0, 0)
+        sort_scales(0)
+        leverage(0, 0)
+        sort_scales(1)
+        later_loads()
         quantize_liq(0, 0, half)
         scalar_bank(0, 0, 0, 0, half)
         scalar_bank(0, 0, 1, 0, half)
         leverage(0, 1)
-        sort_scales(0, 1)
-        quantize_liq(0, half, half)
         sort_codes(0, 1)
+        quantize_liq(0, half, half)
         for i in range(last):
             c, h = divmod(i, HALVES)
             width = SCALAR_COLS[i][1]
             new_drop(i, 0)
+            new_drop(i, 1)
             new_liq(i + 1)
             if i == 0:
-                turn_loss(1, 0)
-                turn_loss(1, 1)
+                sort_codes(1, 0)
                 scalar_bank(0, 0, 0, half, half)
                 scalar_bank(0, 0, 1, half, half)
+                for s0 in range(width, ROWS, P):
+                    vector_bank(i, 1, s0)
+                turn_loss(1, 0)
+                turn_loss(1, 1)
             else:
                 new_pairs(i, 0)
                 scalar_bank(i, 0, 0, 0, ROWS)
                 scalar_bank(i, 0, 1, 0, ROWS)
                 turn_loss(i + 1, 0)
                 turn_loss(i + 1, 1)
+                scalar_bank(i, 0, 2, 0, ROWS)
+                scalar_bank(i, 0, 3, 0, ROWS)
             leverage(i + 1, 0)
             leverage(i + 1, 1)
             if i > 0:
                 quantize_drop(i - 1, 1, 0, ROWS)
-                scalar_bank(i, 0, 2, 0, ROWS)
-                scalar_bank(i, 0, 3, 0, ROWS)
-            if c + 1 < C:
-                sort_scales(c + 1, h)
             quantize_liq(i + 1, 0, ROWS)
-            new_drop(i, 1)
-            if c + 1 < C:
+            if i > 0 and c + 1 < C:
                 sort_codes(c + 1, h)
             join_pairs(i, 0, 0, ROWS)
-            for s0 in range(width, ROWS, P):
-                vector_bank(i, 1, s0)
+            if i > 0:
+                for s0 in range(width, ROWS, P):
+                    vector_bank(i, 1, s0)
             if width:
                 new_pairs(i, 1)
                 for n in range(PACK * width // ROWS):

@@ -197,19 +197,18 @@ def tile_fire_sale_contagion_s14_kernel(
             drop_code[i, g] = work.tile([P, ROWS], U32, name="drop_code", tag="drop_code", bufs=4, align_bytes=64)
             drop_scale[i, g] = work.tile([P, ROWS], U8, name="drop_scale", tag="drop_scale", bufs=4, align_bytes=64)
 
-        def new_pairs(i, g):
-            pairs[i, g] = work.tile([P, 2, ROWS, 2], BF16, name="pairs", tag="pairs", bufs=3, align_bytes=64)
-
         def scalar_bank(i, g, n, s0, width):
             c = i // HALVES
             per_bank = ROWS // width
+            if n == 0:
+                pairs[i, g, s0] = work.tile([P, 2, width, 2], BF16, name="pairs", tag="pairs", bufs=4, align_bytes=64)
             bank = psum_s.tile([P, per_bank, width], F32, name="sales_s", tag="bank")
             slots = SLOT_ORDER[n * per_bank : (n + 1) * per_bank]
             for k, t in enumerate(slots):
                 sales(bank[:, k, :], i, g, t, s0, width)
             for k, t in enumerate(slots):
                 nc.scalar.activation(
-                    out=pairs[i, g][:, t // 2, s0 : s0 + width, t % 2],
+                    out=pairs[i, g, s0][:, t // 2, :, t % 2],
                     in_=bank[:, k, :],
                     func=ACT.Relu,
                     scale=imp_abs[:, c, g, t : t + 1],
@@ -219,7 +218,7 @@ def tile_fire_sale_contagion_s14_kernel(
             c = i // HALVES
             nc.vector.tensor_tensor(
                 out=drop[i, g][:, s0 : s0 + width, :].rearrange("p s (u e) -> p s u e", e=2),
-                in0=pairs[i, g][:, :, s0 : s0 + width, :].rearrange("p u s e -> p s u e"),
+                in0=pairs[i, g, s0][:].rearrange("p u s e -> p s u e"),
                 in1=imp_sign[:, c, g : g + 1, :].rearrange("p o (u e) -> p o u e", e=2).broadcast_to([P, width, 2, 2]),
                 op=ALU.mult,
             )
@@ -245,37 +244,42 @@ def tile_fire_sale_contagion_s14_kernel(
                 in_=drop[i, g][:, s0 : s0 + width, :].rearrange("p s t -> p (s t)"),
             )
 
-        def losses(i, j):
+        def loss_pass(bank, i, j, g, start):
             c = i // HALVES
             cols = slice(j * P, (j + 1) * P)
+            nc.tensor.matmul_mx(
+                out=bank[:],
+                lhsT=drop_code[i, g][:, cols].bitcast(FP8X4),
+                lhsT_scale=drop_scale[i, g][:, cols],
+                rhs=hold_code[c][:, g, :].bitcast(FP4X4),
+                rhs_scale=hold_scale[:, GROUPS * c + g, :],
+                start=start,
+                stop=not start,
+            )
+
+        def losses(i, j):
             bank = psum_s.tile([P, B], F32, name="acc", tag="bank")
-            for g in range(GROUPS):
-                nc.tensor.matmul_mx(
-                    out=bank[:],
-                    lhsT=drop_code[i, g][:, cols].bitcast(FP8X4),
-                    lhsT_scale=drop_scale[i, g][:, cols],
-                    rhs=hold_code[c][:, g, :].bitcast(FP4X4),
-                    rhs_scale=hold_scale[:, GROUPS * c + g, :],
-                    start=(g == 0),
-                    stop=(g == GROUPS - 1),
-                )
+            loss_pass(bank, i, j, 0, True)
+            loss_pass(bank, i, j, 1, False)
             return bank
 
         def out_rows(i):
             c, h = divmod(i, HALVES)
             return out[c, h * ROWS : (h + 1) * ROWS, :].rearrange("(p j) b -> p j b", j=PACK)
 
+        def store_rows(i, j, bank, engine_copy):
+            result = work.tile([P, B], F32, name="result", tag="result", bufs=8)
+            engine_copy(out=result[:], in_=bank[:])
+            nc.sync.dma_start(out=out_rows(i)[:, j, :], in_=result[:])
+
         def second_round(i, part):
-            result = work.tile([P, 2, B], F32, name="result", tag="result", bufs=8)
-            for j in range(2):
-                nc.scalar.copy(out=result[:, j, :], in_=losses(i, 2 * part + j)[:])
-            nc.sync.dma_start(out=out_rows(i)[:, 2 * part : 2 * part + 2, :], in_=result[:])
+            for j in (2 * part, 2 * part + 1):
+                store_rows(i, j, losses(i, j), nc.scalar.copy)
 
         half = ROWS // 2
         last = BLOCKS - 1
 
         new_liq(0)
-        new_pairs(0, 0)
         turn_loss(0, 0)
         turn_loss(0, 1)
         n_rows = C + C * GROUPS
@@ -291,66 +295,65 @@ def tile_fire_sale_contagion_s14_kernel(
         nc.scalar.activation(out=imp_sign[:], in_=imp_t, func=ACT.Sign)
 
         sort_codes(0, 0)
-        sort_scales(0)
         leverage(0, 0)
-        sort_scales(1)
-        later_loads()
+        sort_scales(0)
         quantize_liq(0, 0, half)
         scalar_bank(0, 0, 0, 0, half)
         scalar_bank(0, 0, 1, 0, half)
         leverage(0, 1)
-        sort_codes(0, 1)
+        sort_scales(1)
+        later_loads()
         quantize_liq(0, half, half)
-        for i in range(last):
+        sort_codes(0, 1)
+        new_drop(0, 0)
+        new_drop(0, 1)
+        new_liq(1)
+        scalar_bank(0, 0, 0, half, half)
+        scalar_bank(0, 0, 1, half, half)
+        sort_codes(1, 0)
+        vector_bank(0, 1, 0)
+        turn_loss(1, 0)
+        turn_loss(1, 1)
+        leverage(1, 0)
+        leverage(1, 1)
+        vector_bank(0, 1, P)
+        quantize_liq(1, 0, ROWS)
+        scalar_bank(0, 1, 0, half, half)
+        scalar_bank(0, 1, 1, half, half)
+        join_pairs(0, 0, 0, half)
+        join_pairs(0, 0, half, half)
+        join_pairs(0, 1, half, half)
+        quantize_drop(0, 0, 0, ROWS)
+        for i in range(1, last):
             c, h = divmod(i, HALVES)
             width = SCALAR_COLS[i][1]
             new_drop(i, 0)
             new_drop(i, 1)
             new_liq(i + 1)
-            if i == 0:
-                sort_codes(1, 0)
-                scalar_bank(0, 0, 0, half, half)
-                scalar_bank(0, 0, 1, half, half)
-                for s0 in range(width, ROWS, P):
-                    vector_bank(i, 1, s0)
-                turn_loss(1, 0)
-                turn_loss(1, 1)
-            else:
-                new_pairs(i, 0)
-                scalar_bank(i, 0, 0, 0, ROWS)
-                scalar_bank(i, 0, 1, 0, ROWS)
-                turn_loss(i + 1, 0)
-                turn_loss(i + 1, 1)
-                scalar_bank(i, 0, 2, 0, ROWS)
-                scalar_bank(i, 0, 3, 0, ROWS)
+            scalar_bank(i, 0, 0, 0, ROWS)
+            scalar_bank(i, 0, 1, 0, ROWS)
+            turn_loss(i + 1, 0)
+            turn_loss(i + 1, 1)
+            scalar_bank(i, 0, 2, 0, ROWS)
+            scalar_bank(i, 0, 3, 0, ROWS)
             leverage(i + 1, 0)
             leverage(i + 1, 1)
-            if i > 0:
-                quantize_drop(i - 1, 1, 0, ROWS)
+            quantize_drop(i - 1, 1, 0, ROWS)
             quantize_liq(i + 1, 0, ROWS)
-            if i > 0 and c + 1 < C:
+            if c + 1 < C:
                 sort_codes(c + 1, h)
             join_pairs(i, 0, 0, ROWS)
-            if i > 0:
-                for s0 in range(width, ROWS, P):
-                    vector_bank(i, 1, s0)
+            for s0 in range(width, ROWS, P):
+                vector_bank(i, 1, s0)
             if width:
-                new_pairs(i, 1)
                 for n in range(PACK * width // ROWS):
                     scalar_bank(i, 1, n, 0, width)
             quantize_drop(i, 0, 0, ROWS)
-            if i > 0:
-                second_round(i - 1, 0)
-                second_round(i - 1, 1)
+            second_round(i - 1, 0)
+            second_round(i - 1, 1)
             if width:
                 join_pairs(i, 1, 0, width)
 
-        def final_rows(j, engine_copy):
-            result = work.tile([P, B], F32, name="result", tag="result", bufs=8)
-            engine_copy(out=result[:], in_=losses(last, j)[:])
-            nc.sync.dma_start(out=out_rows(last)[:, j, :], in_=result[:])
-
-        new_pairs(last, 0)
         new_drop(last, 0)
         new_drop(last, 1)
         scalar_bank(last, 0, 0, 0, half)
@@ -370,7 +373,13 @@ def tile_fire_sale_contagion_s14_kernel(
         quantize_drop(last, 1, half, half)
         second_round(last - 1, 1)
         quantize_drop(last, 0, half, half)
-        final_rows(0, nc.scalar.copy)
-        final_rows(1, nc.vector.tensor_copy)
-        final_rows(2, nc.scalar.copy)
-        final_rows(3, nc.vector.tensor_copy)
+        store_rows(last, 0, losses(last, 0), nc.scalar.copy)
+        store_rows(last, 1, losses(last, 1), nc.vector.tensor_copy)
+        banks = {}
+        for j in (2, 3):
+            banks[j] = psum_v.tile([P, B], F32, name="acc", tag="bank")
+            loss_pass(banks[j], last, j, 1, True)
+        for j in (2, 3):
+            loss_pass(banks[j], last, j, 0, False)
+        store_rows(last, 2, banks[2], nc.scalar.copy)
+        store_rows(last, 3, banks[3], nc.vector.tensor_copy)

from contextlib import ExitStack

import concourse.mybir as mybir
from concourse.masks import make_identity

C, S, B, A = 4, 1024, 512, 1024
FLOPS = 2 * C * S * B * A * 2

F32 = mybir.dt.float32
BF16 = mybir.dt.bfloat16
I32 = mybir.dt.int32
U32 = mybir.dt.uint32
U8 = mybir.dt.uint8
FP8X4 = mybir.dt.float8_e4m3fn_x4
FP4X4 = mybir.dt.float4_e2m1fn_x4
ACT = mybir.ActivationFunctionType
ALU = mybir.AluOpType

P = 128
PACK = 4
K_PASS = P * PACK
GROUPS = A // K_PASS
ROWS = 512
HALVES = S // ROWS
BLOCKS = C * HALVES
SLOT_ORDER = (0, 2, 1, 3)
SCALAR_COLS = [(512, 256)] + [(512, 128)] * 6 + [(512, 0)]


def tile_fire_sale_contagion_s14_kernel(
    tc, loss, lev, impact, sell_words, sell_scales, hold_words, hold_scales, out
):
    nc = tc.nc
    with ExitStack() as ctx:
        keep = ctx.enter_context(tc.tile_pool(name="keep", bufs=1))
        work = ctx.enter_context(tc.tile_pool(name="work", bufs=2))
        psum_v = ctx.enter_context(tc.psum_pool(name="psum_v", bufs=4))
        psum_s = ctx.enter_context(tc.psum_pool(name="psum_s", bufs=4))
        ctx.enter_context(tc.manual_schedule())

        loss_rows = {}
        sell_raw = {}
        hold_code = {}

        def load_loss(i, part):
            c, h = divmod(i, HALVES)
            rows = loss[c, h * ROWS : (h + 1) * ROWS, :].rearrange("(p j) b -> p j b", j=PACK)
            t = keep.tile([P, 2, B], BF16, name="loss_%d_%d" % (i, part))
            nc.sync.dma_start(out=t[:], in_=rows[:, 2 * part : 2 * part + 2, :])
            loss_rows[i, part] = t

        def load_sell(c, g):
            t = keep.tile([P, 2 * K_PASS], U8, name="sell_raw_%d_%d" % (c, g), align_bytes=64)
            nc.sync.dma_start(
                out=t[:].bitcast(I32), in_=sell_words[c, :, 2 * K_PASS * g : 2 * K_PASS * (g + 1)].bitcast(I32)
            )
            sell_raw[c, g] = t

        def load_hold(c):
            t = keep.tile([P, GROUPS, 2 * B], U8, name="hold_code_%d" % c, align_bytes=64)
            nc.sync.dma_start(
                out=t[:].bitcast(I32),
                in_=hold_words[GROUPS * c : GROUPS * (c + 1)].rearrange("g p n -> p g n").bitcast(I32),
            )
            hold_code[c] = t

        load_loss(0, 0)
        load_sell(0, 0)
        load_loss(0, 1)
        lev_first = keep.tile([P, 1, PACK], BF16, name="lev_first")
        nc.sync.dma_start(out=lev_first[:, 0, :], in_=lev[0].rearrange("(p t) -> p t", t=PACK))

        ident = keep.tile([P, P], F32, name="ident")
        make_identity(nc, ident[:])

        factor_rows = keep.tile([P, K_PASS], BF16, name="factor_rows")
        sell_scale_raw = keep.tile([P, A], U8, name="sell_scale_raw", align_bytes=64)
        sell_scale_rest = keep.tile([P, C - 1, A], U8, name="sell_scale_rest", align_bytes=64)
        hold_scale = keep.tile([P, C * GROUPS, B], U8, name="hold_scale", align_bytes=64)
        nc.vector.memset(sell_scale_raw[:].bitcast(I32), 0)
        nc.vector.memset(factor_rows[:], 0.0)
        nc.vector.memset(sell_scale_rest[:].bitcast(I32), 0)
        nc.vector.memset(hold_scale[:].bitcast(I32), 0)

        for q in range(4):
            nc.sync.dma_start(
                out=sell_scale_raw[32 * q : 32 * q + 4 * C, :].bitcast(I32),
                in_=sell_scales[:, 4 * q : 4 * q + 4, :].bitcast(I32),
            )
        nc.sync.dma_start(out=factor_rows[0:C, :], in_=lev)
        nc.sync.dma_start(
            out=factor_rows[C : C + C * GROUPS, :], in_=impact.rearrange("c (g k) -> (c g) k", g=GROUPS)
        )
        load_sell(0, 1)
        load_loss(1, 0)
        load_loss(1, 1)
        load_sell(1, 0)
        load_sell(1, 1)
        load_hold(0)
        for q in range(4):
            nc.sync.dma_start(
                out=hold_scale[32 * q : 32 * q + 4, :, :].bitcast(I32),
                in_=hold_scales[:, 4 * q : 4 * q + 4, :].rearrange("g r n -> r g n").bitcast(I32),
            )

        def later_loads():
            for c in range(1, C):
                for q in range(4):
                    nc.sync.dma_start(
                        out=sell_scale_rest[32 * q : 32 * q + 4, c - 1, :].bitcast(I32),
                        in_=sell_scale_all[32 * q + 4 * c : 32 * q + 4 * c + 4, :].bitcast(I32),
                    )
                if c > 1:
                    load_sell(c, 0)
                    load_sell(c, 1)
                for i in range(HALVES * c, HALVES * (c + 1)):
                    load_loss(i, 0)
                    load_loss(i, 1)
                load_hold(c)

        sell_code = {}
        sell_scale_all = keep.tile([P, A], U8, name="sell_scale_all", align_bytes=64)

        def sort_codes(c, g):
            code = keep.tile([P, PACK, 2 * P], U8, name="sell_code_%d_%d" % (c, g), align_bytes=64)
            nc.vector.tensor_copy(
                out=code[:].rearrange("p t (w m b) -> p w t m b", m=8, b=2),
                in_=sell_raw[c, g][:].rearrange("p (w m t b) -> p w t m b", m=8, t=PACK, b=2),
            )
            sell_code[c, g] = code

        def sort_scales(g):
            cols = slice(K_PASS * g, K_PASS * (g + 1))
            nc.vector.tensor_copy(
                out=sell_scale_all[:, cols].rearrange("p (t w m) -> p w t m", t=PACK, m=16),
                in_=sell_scale_raw[:, cols].rearrange("p (w m t) -> p w t m", m=16, t=PACK),
            )

        def sell_scale(c, g, t):
            plane = sell_scale_all[:] if c == 0 else sell_scale_rest[:, c - 1, :]
            return plane[:, K_PASS * g + P * t : K_PASS * g + P * (t + 1)]

        liq = {}
        liq_code = {}
        liq_scale = {}

        def new_liq(i):
            liq[i] = work.tile([P, ROWS, PACK], BF16, name="liq", tag="liq", align_bytes=64)
            liq_code[i] = work.tile([P, ROWS], U32, name="liq_code", tag="liq_code", align_bytes=64)
            liq_scale[i] = work.tile([P, ROWS], U8, name="liq_scale", tag="liq_scale", align_bytes=64)

        turned = {}

        def turn_loss(i, part):
            turned[i, part] = psum_v.tile([P, 2, 2 * P], F32, name="turned", tag="bank")
            for j in range(2):
                words = loss_rows[i, part][:, j, :].bitcast(F32)
                for u in range(2):
                    nc.tensor.transpose(turned[i, part][:, u, j * P : (j + 1) * P], words[:, u : 2 * P : 2], ident[:])

        def leverage(i, part):
            c = i // HALVES
            factor = lev_first[:] if i == 0 else factors[:, c : c + 1, :]
            nc.vector.tensor_tensor(
                out=liq[i][:, 2 * P * part : 2 * P * (part + 1), :].rearrange("p s (u e) -> p s u e", e=2),
                in0=turned[i, part][:].bitcast(BF16).rearrange("p u (s e) -> p s u e", e=2),
                in1=factor.rearrange("p o (u e) -> p o u e", e=2).broadcast_to([P, 2 * P, 2, 2]),
                op=ALU.mult,
            )

        def quantize_liq(i, s0, width):
            nc.vector.quantize_mx(
                out=liq_code[i][:, s0 : s0 + width].bitcast(FP8X4),
                scales=liq_scale[i][:, s0 : s0 + width],
                in_=liq[i][:, s0 : s0 + width, :].rearrange("p s t -> p (s t)"),
            )

        def sales(dst, i, g, t, s0, width):
            c = i // HALVES
            nc.tensor.matmul_mx(
                out=dst,
                lhsT=sell_code[c, g][:, t, :].bitcast(FP4X4),
                lhsT_scale=sell_scale(c, g, t),
                rhs=liq_code[i][:, s0 : s0 + width].bitcast(FP8X4),
                rhs_scale=liq_scale[i][:, s0 : s0 + width],
                start=True,
                stop=True,
            )

        pairs = {}
        drop = {}
        drop_code = {}
        drop_scale = {}

        def new_drop(i, g):
            drop[i, g] = work.tile([P, ROWS, PACK], BF16, name="drop", tag="drop", bufs=4, align_bytes=64)
            drop_code[i, g] = work.tile([P, ROWS], U32, name="drop_code", tag="drop_code", bufs=4, align_bytes=64)
            drop_scale[i, g] = work.tile([P, ROWS], U8, name="drop_scale", tag="drop_scale", bufs=4, align_bytes=64)

        def scalar_bank(i, g, n, s0, width):
            c = i // HALVES
            per_bank = ROWS // width
            if n == 0:
                pairs[i, g, s0] = work.tile([P, 2, width, 2], BF16, name="pairs", tag="pairs", bufs=4, align_bytes=64)
            bank = psum_s.tile([P, per_bank, width], F32, name="sales_s", tag="bank")
            slots = SLOT_ORDER[n * per_bank : (n + 1) * per_bank]
            for k, t in enumerate(slots):
                sales(bank[:, k, :], i, g, t, s0, width)
            for k, t in enumerate(slots):
                nc.scalar.activation(
                    out=pairs[i, g, s0][:, t // 2, :, t % 2],
                    in_=bank[:, k, :],
                    func=ACT.Relu,
                    scale=imp_abs[:, c, g, t : t + 1],
                )

        def join_pairs(i, g, s0, width):
            c = i // HALVES
            nc.vector.tensor_tensor(
                out=drop[i, g][:, s0 : s0 + width, :].rearrange("p s (u e) -> p s u e", e=2),
                in0=pairs[i, g, s0][:].rearrange("p u s e -> p s u e"),
                in1=imp_sign[:, c, g : g + 1, :].rearrange("p o (u e) -> p o u e", e=2).broadcast_to([P, width, 2, 2]),
                op=ALU.mult,
            )

        def vector_bank(i, g, s0):
            c = i // HALVES
            bank = psum_v.tile([P, PACK, P], F32, name="sales_v", tag="bank")
            for t in range(PACK):
                sales(bank[:, t, :], i, g, t, s0, P)
            nc.vector.scalar_tensor_tensor(
                out=drop[i, g][:, s0 : s0 + P, :],
                in0=bank[:].rearrange("p t s -> p s t"),
                scalar=0.0,
                in1=imp_t[:, c, g : g + 1, :].broadcast_to([P, P, PACK]),
                op0=ALU.max,
                op1=ALU.mult,
            )

        def quantize_drop(i, g, s0, width):
            nc.vector.quantize_mx(
                out=drop_code[i, g][:, s0 : s0 + width].bitcast(FP8X4),
                scales=drop_scale[i, g][:, s0 : s0 + width],
                in_=drop[i, g][:, s0 : s0 + width, :].rearrange("p s t -> p (s t)"),
            )

        def loss_pass(bank, i, j, g, start):
            c = i // HALVES
            cols = slice(j * P, (j + 1) * P)
            nc.tensor.matmul_mx(
                out=bank[:],
                lhsT=drop_code[i, g][:, cols].bitcast(FP8X4),
                lhsT_scale=drop_scale[i, g][:, cols],
                rhs=hold_code[c][:, g, :].bitcast(FP4X4),
                rhs_scale=hold_scale[:, GROUPS * c + g, :],
                start=start,
                stop=not start,
            )

        def losses(i, j):
            bank = psum_s.tile([P, B], F32, name="acc", tag="bank")
            loss_pass(bank, i, j, 0, True)
            loss_pass(bank, i, j, 1, False)
            return bank

        def out_rows(i):
            c, h = divmod(i, HALVES)
            return out[c, h * ROWS : (h + 1) * ROWS, :].rearrange("(p j) b -> p j b", j=PACK)

        def store_rows(i, j, bank, engine_copy):
            result = work.tile([P, B], F32, name="result", tag="result", bufs=8)
            engine_copy(out=result[:], in_=bank[:])
            nc.sync.dma_start(out=out_rows(i)[:, j, :], in_=result[:])

        def second_round(i, part):
            for j in (2 * part, 2 * part + 1):
                store_rows(i, j, losses(i, j), nc.scalar.copy)

        half = ROWS // 2
        last = BLOCKS - 1

        new_liq(0)
        turn_loss(0, 0)
        turn_loss(0, 1)
        n_rows = C + C * GROUPS
        factor_bank = psum_s.tile([P, 2, P], F32, name="factor_bank", tag="bank")
        for u in range(2):
            nc.tensor.transpose(factor_bank[:, u, :], factor_rows[:].bitcast(F32)[:, u : 2 * P : 2], ident[:])
        factors = keep.tile([P, n_rows, PACK], BF16, name="factors")
        nc.scalar.copy(out=factors[:].bitcast(F32), in_=factor_bank[:, :, 0:n_rows].rearrange("p u r -> p r u"))
        imp_t = factors[:, C:n_rows, :].rearrange("p (c g) t -> p c g t", g=GROUPS)
        imp_abs = keep.tile([P, C, GROUPS, PACK], F32, name="imp_abs")
        imp_sign = keep.tile([P, C, GROUPS, PACK], BF16, name="imp_sign")
        nc.scalar.activation(out=imp_abs[:], in_=imp_t, func=ACT.Abs)
        nc.scalar.activation(out=imp_sign[:], in_=imp_t, func=ACT.Sign)

        sort_codes(0, 0)
        leverage(0, 0)
        sort_scales(0)
        quantize_liq(0, 0, half)
        scalar_bank(0, 0, 0, 0, half)
        scalar_bank(0, 0, 1, 0, half)
        leverage(0, 1)
        sort_scales(1)
        later_loads()
        quantize_liq(0, half, half)
        sort_codes(0, 1)
        new_drop(0, 0)
        new_drop(0, 1)
        new_liq(1)
        scalar_bank(0, 0, 0, half, half)
        scalar_bank(0, 0, 1, half, half)
        sort_codes(1, 0)
        vector_bank(0, 1, 0)
        turn_loss(1, 0)
        turn_loss(1, 1)
        leverage(1, 0)
        leverage(1, 1)
        vector_bank(0, 1, P)
        quantize_liq(1, 0, ROWS)
        scalar_bank(0, 1, 0, half, half)
        scalar_bank(0, 1, 1, half, half)
        join_pairs(0, 0, 0, half)
        join_pairs(0, 0, half, half)
        join_pairs(0, 1, half, half)
        quantize_drop(0, 0, 0, ROWS)
        for i in range(1, last):
            c, h = divmod(i, HALVES)
            width = SCALAR_COLS[i][1]
            new_drop(i, 0)
            new_drop(i, 1)
            new_liq(i + 1)
            scalar_bank(i, 0, 0, 0, ROWS)
            scalar_bank(i, 0, 1, 0, ROWS)
            turn_loss(i + 1, 0)
            turn_loss(i + 1, 1)
            scalar_bank(i, 0, 2, 0, ROWS)
            scalar_bank(i, 0, 3, 0, ROWS)
            leverage(i + 1, 0)
            leverage(i + 1, 1)
            quantize_drop(i - 1, 1, 0, ROWS)
            quantize_liq(i + 1, 0, ROWS)
            if c + 1 < C:
                sort_codes(c + 1, h)
            join_pairs(i, 0, 0, ROWS)
            for s0 in range(width, ROWS, P):
                vector_bank(i, 1, s0)
            if width:
                for n in range(PACK * width // ROWS):
                    scalar_bank(i, 1, n, 0, width)
            quantize_drop(i, 0, 0, ROWS)
            second_round(i - 1, 0)
            second_round(i - 1, 1)
            if width:
                join_pairs(i, 1, 0, width)

        new_drop(last, 0)
        new_drop(last, 1)
        scalar_bank(last, 0, 0, 0, half)
        scalar_bank(last, 0, 1, 0, half)
        vector_bank(last, 1, 0)
        quantize_drop(last - 1, 1, 0, ROWS)
        vector_bank(last, 1, P)
        scalar_bank(last, 0, 0, half, half)
        scalar_bank(last, 0, 1, half, half)
        join_pairs(last, 0, 0, half)
        quantize_drop(last, 1, 0, half)
        vector_bank(last, 1, 2 * P)
        quantize_drop(last, 0, 0, half)
        vector_bank(last, 1, 3 * P)
        second_round(last - 1, 0)
        join_pairs(last, 0, half, half)
        quantize_drop(last, 1, half, half)
        second_round(last - 1, 1)
        quantize_drop(last, 0, half, half)
        store_rows(last, 0, losses(last, 0), nc.scalar.copy)
        store_rows(last, 1, losses(last, 1), nc.vector.tensor_copy)
        banks = {}
        for j in (2, 3):
            banks[j] = psum_v.tile([P, B], F32, name="acc", tag="bank")
            loss_pass(banks[j], last, j, 1, True)
        for j in (2, 3):
            loss_pass(banks[j], last, j, 0, False)
        store_rows(last, 2, banks[2], nc.scalar.copy)
        store_rows(last, 3, banks[3], nc.vector.tensor_copy)
